import numpy as np
import ml_dtypes


def mxq(x, axis, fmt="e4m3"):
    dtype, down = {"e4m3": (ml_dtypes.float8_e4m3fn, 7), "e5m2": (ml_dtypes.float8_e5m2, 14)}[fmt]
    v = np.moveaxis(np.asarray(x, np.float32).astype(ml_dtypes.bfloat16).astype(np.float64), axis, -1)
    blocks = v.reshape(v.shape[:-1] + (-1, 32))
    amax = np.abs(blocks).max(-1, keepdims=True)
    byte = np.maximum(np.where(amax > 0, np.frexp(amax)[1] - 1 + 127, 0) - down, 1)
    scale = np.exp2(byte - 127.0)
    codes = (blocks / scale).astype(np.float32).astype(dtype).astype(np.float64)
    return np.moveaxis((codes * scale).reshape(v.shape), -1, axis)


WIDE = False


def mx_kscale(k):
    if not WIDE:
        return np.ones(k)
    levels = np.array([10, -10, 5, -5, 0])
    if k % 512:
        return np.exp2(np.random.permutation(np.resize(levels, k // 32))).repeat(32)
    a = np.empty((k // 512, 16))
    for p in range(k // 512):
        a[p, :8] = np.random.permutation(np.resize(levels, 8))
        for g in range(8):
            far = levels[np.abs(levels - a[p, g]) >= 10]
            a[p, g + 8] = far[np.random.randint(len(far))]
    return np.exp2(a.ravel()).repeat(32)


BF16 = ml_dtypes.bfloat16


def bf(x):
    return np.asarray(x, np.float32).astype(BF16)


def f64(x):
    return np.asarray(x).astype(np.float64)


E2M1 = np.array([0.0, 0.5, 1.0, 1.5, 2.0, 3.0, 4.0, 6.0, -0.0, -0.5, -1.0, -1.5, -2.0, -3.0, -4.0, -6.0])


def pack_weight(w, fmt):
    k, n = w.shape
    w = f64(bf(w)).reshape(k // 32, 32, n)
    amax = np.abs(w).max(1)
    if fmt == "e4m3":
        byte = np.frexp(amax)[1] - 1 + 127 - 7
    else:
        mant, ex = np.frexp(amax / 6.0)
        byte = np.where(mant > 0.5, ex, ex - 1) + 127
    byte = np.clip(np.where(amax > 0, byte, 1), 1, 254)
    scaled = (w * np.exp2(127.0 - byte)[:, None, :]).reshape(k, n).astype(np.float32)
    by_word = np.ascontiguousarray(scaled.reshape(k // 512, 128, 4, n).transpose(0, 1, 3, 2))
    if fmt == "e4m3":
        words = by_word.astype(ml_dtypes.float8_e4m3fn).view(np.uint8)
    else:
        c = by_word.astype(ml_dtypes.float4_e2m1fn).view(np.uint8) & 0xF
        words = c[..., 0::2] | (c[..., 1::2] << 4)
    return np.ascontiguousarray(words), np.ascontiguousarray(byte.astype(np.uint8).reshape(k // 512, 16, n))


def unpack_weight(words, scales, fmt):
    g, p, n, _ = words.shape
    if fmt == "e4m3":
        vals = np.ascontiguousarray(words).view(ml_dtypes.float8_e4m3fn).astype(np.float64)
    else:
        nib = np.empty((g, p, n, 4), np.uint8)
        nib[..., 0::2] = words & 0xF
        nib[..., 1::2] = words >> 4
        vals = E2M1[nib]
    vals = vals * np.repeat(np.exp2(scales.astype(np.float64) - 127.0), 8, axis=1)[..., None]
    return vals.transpose(0, 1, 3, 2).reshape(g * 512, n)
def pack4(w):
    words, scales = pack_weight(w, "e2m1")
    return words.reshape(words.shape[0], 128, -1), scales


def unpack4(words, scales):
    return unpack_weight(words.reshape(words.shape[0], 128, -1, 2), scales, "e2m1")


H, M, K, F, N = 4, 512, 1024, 1024, 512


def setup_inputs():
    s, t = mx_kscale(H * K), mx_kscale(H * F)
    force_map = np.random.standard_normal((H, K, F)) / np.sqrt(K) * t.reshape(H, 1, F)
    force_words, force_scales = pack4(force_map.reshape(H * K, F) / s[:, None])
    grasp_words, grasp_scales = pack4(np.random.standard_normal((H * F, N)) / np.sqrt(F) / t[:, None])
    return {"x": bf(np.random.standard_normal((H, M, K)) * s.reshape(H, 1, K)),
            "force_words": force_words,
            "force_scales": force_scales,
            "bias": bf(0.4 * np.random.standard_normal((H, F)) * t.reshape(H, F)),
            "grasp_words": grasp_words,
            "grasp_scales": grasp_scales,
            "wrench": bf(np.random.standard_normal((H, M, N)))}


def reference(x, force_words, force_scales, bias, grasp_words, grasp_scales, wrench):
    wf = unpack4(force_words, force_scales).reshape(H, K, F)
    wg = unpack4(grasp_words, grasp_scales).reshape(H, F, N)
    pre = mxq(f64(x), 2, "e4m3") @ wf
    force = np.maximum(pre + f64(bias)[:, None, :], 0.0)
    applied = mxq(force, 2, "e4m3") @ wg
    residual = applied - f64(wrench)
    cost = np.mean(residual * residual, axis=2)
    return residual, cost

@@ -1,0 +1,238 @@
+import math
+from contextlib import ExitStack
+
+import concourse.mybir as mybir
+from concourse.masks import make_identity
+
+H, M, K, F, N = 4, 512, 1024, 1024, 512
+FLOPS = 2 * H * M * K * F + 2 * H * M * F * N
+
+F32 = mybir.dt.float32
+BF16 = mybir.dt.bfloat16
+I32 = mybir.dt.int32
+U32 = mybir.dt.uint32
+U8 = mybir.dt.uint8
+FP8X4 = mybir.dt.float8_e4m3fn_x4
+FP4X4 = mybir.dt.float4_e2m1fn_x4
+ACT = mybir.ActivationFunctionType
+ALU = mybir.AluOpType
+
+P = 128
+PASS = 512
+G = 2
+TILES_PER_OBJECT = M // P
+TILES = H * TILES_PER_OBJECT
+
+
+def tile_grasp_wrench_residual_s14_kernel(
+    tc, x, force_words, force_scales, bias, grasp_words, grasp_scales, wrench, out_0, out_1
+):
+    nc = tc.nc
+    with ExitStack() as ctx:
+        keep = ctx.enter_context(tc.tile_pool(name="keep", bufs=1))
+        work = ctx.enter_context(tc.tile_pool(name="work", bufs=3))
+        psum = ctx.enter_context(tc.psum_pool(name="psum", bufs=1))
+        ctx.enter_context(tc.manual_schedule())
+
+        ident = keep.tile([P, P], F32, name="ident")
+        x_sb = [keep.tile([P, K], BF16, name="x%d" % n, align_bytes=64) for n in range(TILES)]
+        fw_sb = [keep.tile([P, G, 2 * F], U8, name="fw%d" % h, align_bytes=64) for h in range(H)]
+        gw_sb = [keep.tile([P, G, 2 * N], U8, name="gw%d" % h, align_bytes=64) for h in range(H)]
+        fs_first = keep.tile([P, G, F], U8, name="fs_first", align_bytes=64)
+        fs_rest = keep.tile([P, (H - 1) * G, F], U8, name="fs_rest", align_bytes=64)
+        gs_sb = keep.tile([P, H * G, N], U8, name="gs", align_bytes=64)
+        bias_sb = [keep.tile([P, F], BF16, name="bias%d" % h, align_bytes=64) for h in range(H)]
+        wr_sb = [keep.tile([P, TILES_PER_OBJECT, N], BF16, name="wr%d" % h, align_bytes=64) for h in range(H)]
+        res_sb = [keep.tile([P, N], F32, name="res%d" % n, align_bytes=64) for n in range(TILES)]
+        cost_cols = keep.tile([P, 32], F32, name="cost_cols", align_bytes=64)
+        cost_rows = keep.tile([P, 32], F32, name="cost_rows", align_bytes=64)
+
+        make_identity(nc, ident[:])
+        for plane in (fs_first, gs_sb, fs_rest):
+            nc.vector.memset(plane[:].bitcast(I32), 0)
+        nc.scalar.activation(out=cost_cols[:], in_=ident[:, 0:32], func=ACT.Square, scale=0.0)
+
+        def load_x(n):
+            h, j = divmod(n, TILES_PER_OBJECT)
+            nc.sync.dma_start(out=x_sb[n][:], in_=x[h, j * P : (j + 1) * P, :])
+
+        def load_words(dst, words, h, cols):
+            src = words[G * h : G * (h + 1), :, cols].rearrange("g p c -> p g c")
+            nc.sync.dma_start(out=dst[:, :, cols].bitcast(I32), in_=src.bitcast(I32))
+
+        def load_scales(plane, scales):
+            for r in range(4):
+                src = scales[:, r:16:4, :].rearrange("g q n -> q g n")
+                nc.sync.dma_start(out=plane[r:P:32, :, :].bitcast(I32), in_=src.bitcast(I32))
+
+        def load_bias(h):
+            nc.sync.dma_start(out=bias_sb[h][:], in_=bias[h].partition_broadcast(P))
+
+        def load_wrench(h):
+            nc.sync.dma_start(out=wr_sb[h][:], in_=wrench[h].rearrange("(j p) n -> p j n", p=P))
+
+        load_x(0)
+        load_words(fw_sb[0], force_words, 0, slice(0, F))
+        load_scales(fs_first, force_scales[0:G])
+        load_x(1)
+        load_words(fw_sb[0], force_words, 0, slice(F, 2 * F))
+        load_bias(0)
+        load_x(2)
+        load_words(gw_sb[0], grasp_words, 0, slice(0, 2 * N))
+        load_x(3)
+        load_scales(gs_sb, grasp_scales)
+        load_wrench(0)
+        load_x(4)
+        load_scales(fs_rest, force_scales[G:])
+        for h in range(1, H):
+            first = h * TILES_PER_OBJECT
+            load_words(fw_sb[h], force_words, h, slice(0, 2 * F))
+            load_bias(h)
+            load_x(first + 1)
+            load_x(first + 2)
+            load_words(gw_sb[h], grasp_words, h, slice(0, 2 * N))
+            load_wrench(h)
+            load_x(first + 3)
+            if h + 1 < H:
+                load_x(first + 4)
+
+        xt = {}
+        xg = {}
+        xq = {}
+        pre = {}
+        fb = {}
+        ft = {}
+        fg = {}
+        fq = {}
+        acc = {}
+
+        def force_scale(h, g):
+            return fs_first[:, g, :] if h == 0 else fs_rest[:, G * (h - 1) + g, :]
+
+        def transpose_x(n):
+            words = x_sb[n][:].bitcast(F32)
+            xt[n] = psum.tile([P, G, 2, P], F32, name="xt", bufs=2)
+            for g in range(G):
+                for u in range(2):
+                    nc.tensor.transpose(xt[n][:, g, u, :], words[:, 256 * g + u : 256 * (g + 1) : 2], ident[:])
+
+        def copy_x(n):
+            xg[n] = work.tile([P, K], BF16, name="xg", align_bytes=64)
+            nc.scalar.copy(
+                out=xg[n][:].bitcast(F32).rearrange("p (g r u) -> p g r u", g=G, u=2),
+                in_=xt[n][:].rearrange("p g u r -> p g r u"),
+            )
+
+        def quantize(src, tag, groups):
+            codes = work.tile([P, G * P], U32, name=tag + "_codes", align_bytes=64)
+            scales = work.tile([P, G * P], U8, name=tag + "_scales", align_bytes=64)
+            for lo, hi in groups:
+                nc.vector.quantize_mx(
+                    out=codes[:, lo * P : hi * P].bitcast(FP8X4),
+                    scales=scales[:, lo * P : hi * P],
+                    in_=src[:, lo * PASS : hi * PASS],
+                )
+            return codes, scales
+
+        def quantize_x(n):
+            xq[n] = quantize(xg[n], "xq", [(0, G)])
+
+        def matmul_force(n):
+            h = n // TILES_PER_OBJECT
+            codes, scales = xq[n]
+            for c in range(G):
+                pre[n, c] = psum.tile([P, PASS], F32, name="pre", bufs=3)
+                for g in range(G):
+                    nc.tensor.matmul_mx(
+                        out=pre[n, c][:],
+                        lhsT=codes[:, g * P : (g + 1) * P].bitcast(FP8X4),
+                        lhsT_scale=scales[:, g * P : (g + 1) * P],
+                        rhs=fw_sb[h][:, g, 2 * PASS * c : 2 * PASS * (c + 1)].bitcast(FP4X4),
+                        rhs_scale=force_scale(h, g)[:, PASS * c : PASS * (c + 1)],
+                        start=(g == 0),
+                        stop=(g == G - 1),
+                    )
+
+        def add_bias(n):
+            h = n // TILES_PER_OBJECT
+            for c in range(G):
+                fb[n, c] = work.tile([P, PASS], BF16, name="fb", align_bytes=64, bufs=4)
+                nc.vector.tensor_tensor(
+                    out=fb[n, c][:].rearrange("t (u p e) -> t u p e", u=2, e=2),
+                    in0=pre[n, c][:].rearrange("t (p u e) -> t u p e", u=2, e=2),
+                    in1=bias_sb[h][:, PASS * c : PASS * (c + 1)].rearrange("t (p u e) -> t u p e", u=2, e=2),
+                    op=ALU.add,
+                )
+
+        def transpose_force(n):
+            for c in range(G):
+                words = fb[n, c][:].bitcast(F32)
+                ft[n, c] = psum.tile([P, 2, P], F32, name="ft", bufs=2)
+                for u in range(2):
+                    nc.tensor.transpose(ft[n, c][:, u, :], words[:, P * u : P * (u + 1)], ident[:])
+
+        def relu_force(n):
+            fg[n] = work.tile([P, F], BF16, name="fg", align_bytes=64)
+            for c in range(G):
+                nc.scalar.activation(
+                    out=fg[n][:, PASS * c : PASS * (c + 1)].rearrange("p (r u e) -> p r u e", u=2, e=2),
+                    in_=ft[n, c][:].rearrange("p u r -> p (u r)").bitcast(BF16).rearrange("p (u r e) -> p r u e", u=2, e=2),
+                    func=ACT.Relu,
+                )
+
+        def quantize_force(n):
+            fq[n] = quantize(fg[n], "fq", [(0, 1), (1, 2)] if n == TILES - 1 else [(0, G)])
+
+        def matmul_wrench(n):
+            h = n // TILES_PER_OBJECT
+            codes, scales = fq[n]
+            acc[n] = psum.tile([P, N], F32, name="acc", bufs=1)
+            for g in range(G):
+                nc.tensor.matmul_mx(
+                    out=acc[n][:],
+                    lhsT=codes[:, g * P : (g + 1) * P].bitcast(FP8X4),
+                    lhsT_scale=scales[:, g * P : (g + 1) * P],
+                    rhs=gw_sb[h][:, g, :].bitcast(FP4X4),
+                    rhs_scale=gs_sb[:, G * h + g, :],
+                    start=(g == 0),
+                    stop=(g == G - 1),
+                )
+
+        def residual(n):
+            h, j = divmod(n, TILES_PER_OBJECT)
+            nc.vector.tensor_tensor(out=res_sb[n][:], in0=acc[n][:], in1=wr_sb[h][:, j, :], op=ALU.subtract)
+            nc.sync.dma_start(out=out_0[h, j * P : (j + 1) * P, :], in_=res_sb[n][:])
+
+        def square_sum(n):
+            squares = work.tile([P, N], BF16, name="squares", align_bytes=64)
+            nc.scalar.activation(
+                out=squares[:],
+                in_=res_sb[n][:],
+                func=ACT.Square,
+                scale=math.sqrt(1.0 / N),
+                accum_out=cost_cols[:, n : n + 1],
+            )
+
+        steps = [
+            (transpose_x, 1),
+            (transpose_force, -1),
+            (copy_x, 1),
+            (relu_force, -1),
+            (square_sum, -3),
+            (quantize_x, 1),
+            (matmul_force, 0),
+            (add_bias, 0),
+            (matmul_wrench, -2),
+            (residual, -2),
+            (quantize_force, -1),
+        ]
+        for it in range(-1, TILES + 3):
+            for step, lead in steps:
+                if 0 <= it + lead < TILES:
+                    step(it + lead)
+
+        nc.vector.transpose(cost_rows[:], cost_cols[:])
+        cost_out = out_1.rearrange("h (j t) -> (h j) t", t=P)
+        for b in range(4):
+            queue = nc.sync if b % 2 == 0 else nc.scalar
+            queue.dma_start(out=cost_out[:, 32 * b : 32 * (b + 1)], in_=cost_rows[32 * b : 32 * b + TILES, :])

@@ -42,11 +42,17 @@ def tile_grasp_wrench_residual_s14_kernel(
         fs_rest = keep.tile([P, (H - 1) * G, F], U8, name="fs_rest", align_bytes=64)
         gs_sb = keep.tile([P, H * G, N], U8, name="gs", align_bytes=64)
         bias_sb = [keep.tile([P, F], BF16, name="bias%d" % h, align_bytes=64) for h in range(H)]
+        bw_first = keep.tile([P, G, 2], F32, name="bw_first", align_bytes=64)
+        bw_rest = keep.tile([P, (H - 1) * G, 2], F32, name="bw_rest", align_bytes=64)
         wr_sb = [keep.tile([P, TILES_PER_OBJECT, N], BF16, name="wr%d" % h, align_bytes=64) for h in range(H)]
         res_sb = [keep.tile([P, N], F32, name="res%d" % n, align_bytes=64) for n in range(TILES)]
         cost_cols = keep.tile([P, 32], F32, name="cost_cols", align_bytes=64)
         cost_rows = keep.tile([P, 32], F32, name="cost_rows", align_bytes=64)
 
+        def load_bias(queue, dst, rows):
+            queue.dma_start(out=dst[:], in_=rows.bitcast(F32).rearrange("h (c p u) -> p (h c) u", c=G, u=2))
+
+        load_bias(nc.scalar, bw_first, bias[0:1, :])
         make_identity(nc, ident[:])
         for plane in (fs_first, gs_sb, fs_rest):
             nc.vector.memset(plane[:].bitcast(I32), 0)
@@ -65,9 +71,6 @@ def tile_grasp_wrench_residual_s14_kernel(
                 src = scales[:, r:16:4, :].rearrange("g q n -> q g n")
                 nc.sync.dma_start(out=plane[r:P:32, :, :].bitcast(I32), in_=src.bitcast(I32))
 
-        def load_bias(h):
-            nc.sync.dma_start(out=bias_sb[h][:], in_=bias[h].partition_broadcast(P))
-
         def load_wrench(h):
             nc.sync.dma_start(out=wr_sb[h][:], in_=wrench[h].rearrange("(j p) n -> p j n", p=P))
 
@@ -76,7 +79,7 @@ def tile_grasp_wrench_residual_s14_kernel(
         load_scales(fs_first, force_scales[0:G])
         load_x(1)
         load_words(fw_sb[0], force_words, 0, slice(F, 2 * F))
-        load_bias(0)
+        load_bias(nc.sync, bw_rest, bias[1:, :])
         load_x(2)
         load_words(gw_sb[0], grasp_words, 0, slice(0, 2 * N))
         load_x(3)
@@ -87,7 +90,6 @@ def tile_grasp_wrench_residual_s14_kernel(
         for h in range(1, H):
             first = h * TILES_PER_OBJECT
             load_words(fw_sb[h], force_words, h, slice(0, 2 * F))
-            load_bias(h)
             load_x(first + 1)
             load_x(first + 2)
             load_words(gw_sb[h], grasp_words, h, slice(0, 2 * N))
@@ -96,6 +98,7 @@ def tile_grasp_wrench_residual_s14_kernel(
             if h + 1 < H:
                 load_x(first + 4)
 
+        bt = {}
         xt = {}
         xg = {}
         xq = {}
@@ -109,19 +112,43 @@ def tile_grasp_wrench_residual_s14_kernel(
         def force_scale(h, g):
             return fs_first[:, g, :] if h == 0 else fs_rest[:, G * (h - 1) + g, :]
 
+        whole = [(0, G)]
+        by_pass = [(0, 1), (1, 2)]
+
+        def x_groups(n):
+            return by_pass if n == 0 else whole
+
+        def force_groups(n):
+            return by_pass if n == TILES - 1 else whole
+
+        def transpose_bias(h):
+            bt[h] = psum.tile([P, G, 2, P], F32, name="acc", bufs=2)
+            words = bw_first[:] if h == 0 else bw_rest[:, G * (h - 1) : G * h, :]
+            for c in range(G):
+                for u in range(2):
+                    column = words[:, c, u : u + 1].to_broadcast([P, P])
+                    nc.tensor.transpose(bt[h][:, c, u, :], column, ident[:])
+
+        def copy_bias(h):
+            nc.scalar.copy(out=bias_sb[h][:].bitcast(F32), in_=bt[h][:].rearrange("t c u p -> t (c u p)"))
+
         def transpose_x(n):
             words = x_sb[n][:].bitcast(F32)
-            xt[n] = psum.tile([P, G, 2, P], F32, name="xt", bufs=2)
-            for g in range(G):
-                for u in range(2):
-                    nc.tensor.transpose(xt[n][:, g, u, :], words[:, 256 * g + u : 256 * (g + 1) : 2], ident[:])
+            for lo, hi in x_groups(n):
+                xt[n, lo] = psum.tile([P, 2, hi - lo, P], F32, name="tp", bufs=3)
+                for g in range(lo, hi):
+                    for u in range(2):
+                        nc.tensor.transpose(
+                            xt[n, lo][:, u, g - lo, :], words[:, 256 * g + u : 256 * (g + 1) : 2], ident[:]
+                        )
 
         def copy_x(n):
             xg[n] = work.tile([P, K], BF16, name="xg", align_bytes=64)
-            nc.scalar.copy(
-                out=xg[n][:].bitcast(F32).rearrange("p (g r u) -> p g r u", g=G, u=2),
-                in_=xt[n][:].rearrange("p g u r -> p g r u"),
-            )
+            for lo, hi in x_groups(n):
+                nc.scalar.copy(
+                    out=xg[n][:, PASS * lo : PASS * hi].bitcast(F32).rearrange("p (w u) -> p w u", u=2),
+                    in_=xt[n, lo][:].rearrange("p u g r -> p (g r) u"),
+                )
 
         def quantize(src, tag, groups):
             codes = work.tile([P, G * P], U32, name=tag + "_codes", align_bytes=64)
@@ -135,7 +162,7 @@ def tile_grasp_wrench_residual_s14_kernel(
             return codes, scales
 
         def quantize_x(n):
-            xq[n] = quantize(xg[n], "xq", [(0, G)])
+            xq[n] = quantize(xg[n], "xq", x_groups(n))
 
         def matmul_force(n):
             h = n // TILES_PER_OBJECT
@@ -160,33 +187,35 @@ def tile_grasp_wrench_residual_s14_kernel(
                 nc.vector.tensor_tensor(
                     out=fb[n, c][:].rearrange("t (u p e) -> t u p e", u=2, e=2),
                     in0=pre[n, c][:].rearrange("t (p u e) -> t u p e", u=2, e=2),
-                    in1=bias_sb[h][:, PASS * c : PASS * (c + 1)].rearrange("t (p u e) -> t u p e", u=2, e=2),
+                    in1=bias_sb[h][:, PASS * c : PASS * (c + 1)].rearrange("t (u p e) -> t u p e", u=2, e=2),
                     op=ALU.add,
                 )
 
         def transpose_force(n):
-            for c in range(G):
-                words = fb[n, c][:].bitcast(F32)
-                ft[n, c] = psum.tile([P, 2, P], F32, name="ft", bufs=2)
-                for u in range(2):
-                    nc.tensor.transpose(ft[n, c][:, u, :], words[:, P * u : P * (u + 1)], ident[:])
+            for lo, hi in force_groups(n):
+                ft[n, lo] = psum.tile([P, 2, hi - lo, P], F32, name="tp", bufs=3)
+                for c in range(lo, hi):
+                    words = fb[n, c][:].bitcast(F32)
+                    for u in range(2):
+                        nc.tensor.transpose(ft[n, lo][:, u, c - lo, :], words[:, P * u : P * (u + 1)], ident[:])
 
         def relu_force(n):
             fg[n] = work.tile([P, F], BF16, name="fg", align_bytes=64)
-            for c in range(G):
+            for lo, hi in force_groups(n):
+                pairs = ft[n, lo][:].rearrange("p u c r -> p (u c r)").bitcast(BF16)
                 nc.scalar.activation(
-                    out=fg[n][:, PASS * c : PASS * (c + 1)].rearrange("p (r u e) -> p r u e", u=2, e=2),
-                    in_=ft[n, c][:].rearrange("p u r -> p (u r)").bitcast(BF16).rearrange("p (u r e) -> p r u e", u=2, e=2),
+                    out=fg[n][:, PASS * lo : PASS * hi].rearrange("p (w u e) -> p w u e", u=2, e=2),
+                    in_=pairs.rearrange("p (u w e) -> p w u e", u=2, e=2),
                     func=ACT.Relu,
                 )
 
         def quantize_force(n):
-            fq[n] = quantize(fg[n], "fq", [(0, 1), (1, 2)] if n == TILES - 1 else [(0, G)])
+            fq[n] = quantize(fg[n], "fq", force_groups(n))
 
         def matmul_wrench(n):
             h = n // TILES_PER_OBJECT
             codes, scales = fq[n]
-            acc[n] = psum.tile([P, N], F32, name="acc", bufs=1)
+            acc[n] = psum.tile([P, N], F32, name="acc", bufs=2)
             for g in range(G):
                 nc.tensor.matmul_mx(
                     out=acc[n][:],
@@ -213,23 +242,28 @@ def tile_grasp_wrench_residual_s14_kernel(
                 accum_out=cost_cols[:, n : n + 1],
             )
 
-        steps = [
-            (transpose_x, 1),
-            (transpose_force, -1),
-            (copy_x, 1),
-            (relu_force, -1),
-            (square_sum, -3),
-            (quantize_x, 1),
-            (matmul_force, 0),
-            (add_bias, 0),
-            (matmul_wrench, -2),
-            (residual, -2),
-            (quantize_force, -1),
-        ]
+        bias_at = {-1: 0, 1: 1, 2: 2, 3: 3}
+
+        def at(step, n):
+            if 0 <= n < TILES:
+                step(n)
+
         for it in range(-1, TILES + 3):
-            for step, lead in steps:
-                if 0 <= it + lead < TILES:
-                    step(it + lead)
+            at(transpose_x, it + 1)
+            if it in bias_at:
+                transpose_bias(bias_at[it])
+            at(transpose_force, it - 1)
+            at(copy_x, it + 1)
+            if it in bias_at:
+                copy_bias(bias_at[it])
+            at(relu_force, it - 1)
+            at(square_sum, it - 3)
+            at(quantize_x, it + 1)
+            at(matmul_force, it)
+            at(add_bias, it)
+            at(matmul_wrench, it - 2)
+            at(quantize_force, it - 1)
+            at(residual, it - 2)
 
         nc.vector.transpose(cost_rows[:], cost_cols[:])
         cost_out = out_1.rearrange("h (j t) -> (h j) t", t=P)

@@ -30,7 +30,7 @@ def tile_grasp_wrench_residual_s14_kernel(
     nc = tc.nc
     with ExitStack() as ctx:
         keep = ctx.enter_context(tc.tile_pool(name="keep", bufs=1))
-        work = ctx.enter_context(tc.tile_pool(name="work", bufs=3))
+        work = ctx.enter_context(tc.tile_pool(name="work", bufs=6))
         psum = ctx.enter_context(tc.psum_pool(name="psum", bufs=1))
         ctx.enter_context(tc.manual_schedule())
 
@@ -38,9 +38,17 @@ def tile_grasp_wrench_residual_s14_kernel(
         x_sb = [keep.tile([P, K], BF16, name="x%d" % n, align_bytes=64) for n in range(TILES)]
         fw_sb = [keep.tile([P, G, 2 * F], U8, name="fw%d" % h, align_bytes=64) for h in range(H)]
         gw_sb = [keep.tile([P, G, 2 * N], U8, name="gw%d" % h, align_bytes=64) for h in range(H)]
-        fs_first = keep.tile([P, G, F], U8, name="fs_first", align_bytes=64)
-        fs_rest = keep.tile([P, (H - 1) * G, F], U8, name="fs_rest", align_bytes=64)
-        gs_sb = keep.tile([P, H * G, N], U8, name="gs", align_bytes=64)
+        fs_spans = [(0, 1), (1, 2), (2, H)]
+        gs_spans = [(0, 1), (1, H)]
+        fs_sb = [keep.tile([P, G * (hi - lo), F], U8, name="fs%d" % lo, align_bytes=64) for lo, hi in fs_spans]
+        gs_sb = [keep.tile([P, G * (hi - lo), N], U8, name="gs%d" % lo, align_bytes=64) for lo, hi in gs_spans]
+        banks = [psum.tile([P, PASS], F32, name="bank%d" % b) for b in range(8)]
+        taken = []
+
+        def next_bank():
+            taken.append(banks[len(taken) % len(banks)])
+            return taken[-1]
+
         bias_sb = [keep.tile([P, F], BF16, name="bias%d" % h, align_bytes=64) for h in range(H)]
         bw_first = keep.tile([P, G, 2], F32, name="bw_first", align_bytes=64)
         bw_rest = keep.tile([P, (H - 1) * G, 2], F32, name="bw_rest", align_bytes=64)
@@ -54,7 +62,7 @@ def tile_grasp_wrench_residual_s14_kernel(
 
         load_bias(nc.scalar, bw_first, bias[0:1, :])
         make_identity(nc, ident[:])
-        for plane in (fs_first, gs_sb, fs_rest):
+        for plane in (fs_sb[0], gs_sb[0], fs_sb[1], gs_sb[1], fs_sb[2]):
             nc.vector.memset(plane[:].bitcast(I32), 0)
         nc.scalar.activation(out=cost_cols[:], in_=ident[:, 0:32], func=ACT.Square, scale=0.0)
 
@@ -66,37 +74,42 @@ def tile_grasp_wrench_residual_s14_kernel(
             src = words[G * h : G * (h + 1), :, cols].rearrange("g p c -> p g c")
             nc.sync.dma_start(out=dst[:, :, cols].bitcast(I32), in_=src.bitcast(I32))
 
-        def load_scales(plane, scales):
+        def load_scales(planes, spans, scales, i):
+            lo, hi = spans[i]
             for r in range(4):
-                src = scales[:, r:16:4, :].rearrange("g q n -> q g n")
-                nc.sync.dma_start(out=plane[r:P:32, :, :].bitcast(I32), in_=src.bitcast(I32))
+                src = scales[G * lo : G * hi, r:16:4, :].rearrange("g q n -> q g n")
+                nc.sync.dma_start(out=planes[i][r:P:32, :, :].bitcast(I32), in_=src.bitcast(I32))
 
         def load_wrench(h):
             nc.sync.dma_start(out=wr_sb[h][:], in_=wrench[h].rearrange("(j p) n -> p j n", p=P))
 
         load_x(0)
-        load_words(fw_sb[0], force_words, 0, slice(0, F))
-        load_scales(fs_first, force_scales[0:G])
         load_x(1)
+        load_words(fw_sb[0], force_words, 0, slice(0, F))
+        load_scales(fs_sb, fs_spans, force_scales, 0)
         load_words(fw_sb[0], force_words, 0, slice(F, 2 * F))
-        load_bias(nc.sync, bw_rest, bias[1:, :])
         load_x(2)
-        load_words(gw_sb[0], grasp_words, 0, slice(0, 2 * N))
+        load_bias(nc.sync, bw_rest, bias[1:, :])
         load_x(3)
-        load_scales(gs_sb, grasp_scales)
-        load_wrench(0)
         load_x(4)
-        load_scales(fs_rest, force_scales[G:])
+        load_words(gw_sb[0], grasp_words, 0, slice(0, 2 * N))
+        load_scales(gs_sb, gs_spans, grasp_scales, 0)
+        load_scales(fs_sb, fs_spans, force_scales, 1)
+        load_wrench(0)
+        load_x(5)
+        load_x(6)
+        load_words(fw_sb[1], force_words, 1, slice(0, 2 * F))
+        load_x(7)
+        load_x(8)
+        load_scales(gs_sb, gs_spans, grasp_scales, 1)
+        load_scales(fs_sb, fs_spans, force_scales, 2)
         for h in range(1, H):
-            first = h * TILES_PER_OBJECT
-            load_words(fw_sb[h], force_words, h, slice(0, 2 * F))
-            load_x(first + 1)
-            load_x(first + 2)
             load_words(gw_sb[h], grasp_words, h, slice(0, 2 * N))
             load_wrench(h)
-            load_x(first + 3)
             if h + 1 < H:
-                load_x(first + 4)
+                load_words(fw_sb[h + 1], force_words, h + 1, slice(0, 2 * F))
+            for n in range(4 * h + 5, min(4 * h + 9, TILES)):
+                load_x(n)
 
         bt = {}
         xt = {}
@@ -109,8 +122,13 @@ def tile_grasp_wrench_residual_s14_kernel(
         fq = {}
         acc = {}
 
-        def force_scale(h, g):
-            return fs_first[:, g, :] if h == 0 else fs_rest[:, G * (h - 1) + g, :]
+        def plane_of(planes, spans, h, g):
+            i = max(i for i, (lo, hi) in enumerate(spans) if lo <= h)
+            return planes[i][:, G * (h - spans[i][0]) + g, :]
+
+        def take_bank(passes):
+            bank = next_bank()
+            return bank[:, 0 : 2 * passes * P].rearrange("p (u g r) -> p u g r", u=2, g=passes)
 
         whole = [(0, G)]
         by_pass = [(0, 1), (1, 2)]
@@ -122,20 +140,20 @@ def tile_grasp_wrench_residual_s14_kernel(
             return by_pass if n == TILES - 1 else whole
 
         def transpose_bias(h):
-            bt[h] = psum.tile([P, G, 2, P], F32, name="acc", bufs=2)
+            bt[h] = next_bank()
             words = bw_first[:] if h == 0 else bw_rest[:, G * (h - 1) : G * h, :]
             for c in range(G):
                 for u in range(2):
                     column = words[:, c, u : u + 1].to_broadcast([P, P])
-                    nc.tensor.transpose(bt[h][:, c, u, :], column, ident[:])
+                    nc.tensor.transpose(bt[h][:, (2 * c + u) * P : (2 * c + u + 1) * P], column, ident[:])
 
         def copy_bias(h):
-            nc.scalar.copy(out=bias_sb[h][:].bitcast(F32), in_=bt[h][:].rearrange("t c u p -> t (c u p)"))
+            nc.scalar.copy(out=bias_sb[h][:].bitcast(F32), in_=bt[h][:])
 
         def transpose_x(n):
             words = x_sb[n][:].bitcast(F32)
             for lo, hi in x_groups(n):
-                xt[n, lo] = psum.tile([P, 2, hi - lo, P], F32, name="tp", bufs=3)
+                xt[n, lo] = take_bank(hi - lo)
                 for g in range(lo, hi):
                     for u in range(2):
                         nc.tensor.transpose(
@@ -147,7 +165,7 @@ def tile_grasp_wrench_residual_s14_kernel(
             for lo, hi in x_groups(n):
                 nc.scalar.copy(
                     out=xg[n][:, PASS * lo : PASS * hi].bitcast(F32).rearrange("p (w u) -> p w u", u=2),
-                    in_=xt[n, lo][:].rearrange("p u g r -> p (g r) u"),
+                    in_=xt[n, lo].rearrange("p u g r -> p (g r) u"),
                 )
 
         def quantize(src, tag, groups):
@@ -168,14 +186,14 @@ def tile_grasp_wrench_residual_s14_kernel(
             h = n // TILES_PER_OBJECT
             codes, scales = xq[n]
             for c in range(G):
-                pre[n, c] = psum.tile([P, PASS], F32, name="pre", bufs=3)
+                pre[n, c] = next_bank()
                 for g in range(G):
                     nc.tensor.matmul_mx(
                         out=pre[n, c][:],
                         lhsT=codes[:, g * P : (g + 1) * P].bitcast(FP8X4),
                         lhsT_scale=scales[:, g * P : (g + 1) * P],
                         rhs=fw_sb[h][:, g, 2 * PASS * c : 2 * PASS * (c + 1)].bitcast(FP4X4),
-                        rhs_scale=force_scale(h, g)[:, PASS * c : PASS * (c + 1)],
+                        rhs_scale=plane_of(fs_sb, fs_spans, h, g)[:, PASS * c : PASS * (c + 1)],
                         start=(g == 0),
                         stop=(g == G - 1),
                     )
@@ -183,7 +201,7 @@ def tile_grasp_wrench_residual_s14_kernel(
         def add_bias(n):
             h = n // TILES_PER_OBJECT
             for c in range(G):
-                fb[n, c] = work.tile([P, PASS], BF16, name="fb", align_bytes=64, bufs=4)
+                fb[n, c] = work.tile([P, PASS], BF16, name="fb", align_bytes=64, bufs=8)
                 nc.vector.tensor_tensor(
                     out=fb[n, c][:].rearrange("t (u p e) -> t u p e", u=2, e=2),
                     in0=pre[n, c][:].rearrange("t (p u e) -> t u p e", u=2, e=2),
@@ -193,7 +211,7 @@ def tile_grasp_wrench_residual_s14_kernel(
 
         def transpose_force(n):
             for lo, hi in force_groups(n):
-                ft[n, lo] = psum.tile([P, 2, hi - lo, P], F32, name="tp", bufs=3)
+                ft[n, lo] = take_bank(hi - lo)
                 for c in range(lo, hi):
                     words = fb[n, c][:].bitcast(F32)
                     for u in range(2):
@@ -202,7 +220,7 @@ def tile_grasp_wrench_residual_s14_kernel(
         def relu_force(n):
             fg[n] = work.tile([P, F], BF16, name="fg", align_bytes=64)
             for lo, hi in force_groups(n):
-                pairs = ft[n, lo][:].rearrange("p u c r -> p (u c r)").bitcast(BF16)
+                pairs = ft[n, lo].rearrange("p u c r -> p (u c r)").bitcast(BF16)
                 nc.scalar.activation(
                     out=fg[n][:, PASS * lo : PASS * hi].rearrange("p (w u e) -> p w u e", u=2, e=2),
                     in_=pairs.rearrange("p (u w e) -> p w u e", u=2, e=2),
@@ -215,14 +233,14 @@ def tile_grasp_wrench_residual_s14_kernel(
         def matmul_wrench(n):
             h = n // TILES_PER_OBJECT
             codes, scales = fq[n]
-            acc[n] = psum.tile([P, N], F32, name="acc", bufs=2)
+            acc[n] = next_bank()
             for g in range(G):
                 nc.tensor.matmul_mx(
                     out=acc[n][:],
                     lhsT=codes[:, g * P : (g + 1) * P].bitcast(FP8X4),
                     lhsT_scale=scales[:, g * P : (g + 1) * P],
                     rhs=gw_sb[h][:, g, :].bitcast(FP4X4),
-                    rhs_scale=gs_sb[:, G * h + g, :],
+                    rhs_scale=plane_of(gs_sb, gs_spans, h, g),
                     start=(g == 0),
                     stop=(g == G - 1),
                 )
@@ -244,11 +262,14 @@ def tile_grasp_wrench_residual_s14_kernel(
 
         bias_at = {-1: 0, 1: 1, 2: 2, 3: 3}
 
-        def at(step, n):
-            if 0 <= n < TILES:
-                step(n)
+        rounds = [[0], [1], [2]] + [[n, n + 1] for n in range(3, TILES - 3, 2)] + [[TILES - 3], [TILES - 2], [TILES - 1]]
 
-        for it in range(-1, TILES + 3):
+        def at(step, r):
+            if 0 <= r < len(rounds):
+                for n in rounds[r]:
+                    step(n)
+
+        for it in range(-1, len(rounds) + 3):
             at(transpose_x, it + 1)
             if it in bias_at:
                 transpose_bias(bias_at[it])
@@ -259,8 +280,9 @@ def tile_grasp_wrench_residual_s14_kernel(
             at(relu_force, it - 1)
             at(square_sum, it - 3)
             at(quantize_x, it + 1)
-            at(matmul_force, it)
-            at(add_bias, it)
+            for n in rounds[it] if 0 <= it < len(rounds) else []:
+                matmul_force(n)
+                add_bias(n)
             at(matmul_wrench, it - 2)
             at(quantize_force, it - 1)
             at(residual, it - 2)

@@ -19,9 +19,29 @@ ALU = mybir.AluOpType
 
 P = 128
 PASS = 512
-G = 2
+PASSES = 2
+PAIRS = PASS // 2
+QUADRANT = 32
+SCALE_ROWS = 4
+BANKS = 8
 TILES_PER_OBJECT = M // P
 TILES = H * TILES_PER_OBJECT
+
+SINGLE_ROUNDS_FIRST = 3
+ROUNDS = (
+    [[n] for n in range(SINGLE_ROUNDS_FIRST)]
+    + [[n, n + 1] for n in range(SINGLE_ROUNDS_FIRST, TILES - 1, 2)]
+    + [[TILES - 1]]
+)
+
+FORCE_SCALE_SPANS = [(0, 1), (1, 2), (2, H)]
+GRASP_SCALE_SPANS = [(0, 1), (1, H)]
+
+WORK_BUFS = 6
+SUM_BUFS = 8
+
+BOTH_PASSES = [(0, PASSES)]
+PASS_BY_PASS = [(g, g + 1) for g in range(PASSES)]
 
 
 def tile_grasp_wrench_residual_s14_kernel(
@@ -30,265 +50,254 @@ def tile_grasp_wrench_residual_s14_kernel(
     nc = tc.nc
     with ExitStack() as ctx:
         keep = ctx.enter_context(tc.tile_pool(name="keep", bufs=1))
-        work = ctx.enter_context(tc.tile_pool(name="work", bufs=6))
+        work = ctx.enter_context(tc.tile_pool(name="work", bufs=WORK_BUFS))
         psum = ctx.enter_context(tc.psum_pool(name="psum", bufs=1))
         ctx.enter_context(tc.manual_schedule())
 
-        ident = keep.tile([P, P], F32, name="ident")
-        x_sb = [keep.tile([P, K], BF16, name="x%d" % n, align_bytes=64) for n in range(TILES)]
-        fw_sb = [keep.tile([P, G, 2 * F], U8, name="fw%d" % h, align_bytes=64) for h in range(H)]
-        gw_sb = [keep.tile([P, G, 2 * N], U8, name="gw%d" % h, align_bytes=64) for h in range(H)]
-        fs_spans = [(0, 1), (1, 2), (2, H)]
-        gs_spans = [(0, 1), (1, H)]
-        fs_sb = [keep.tile([P, G * (hi - lo), F], U8, name="fs%d" % lo, align_bytes=64) for lo, hi in fs_spans]
-        gs_sb = [keep.tile([P, G * (hi - lo), N], U8, name="gs%d" % lo, align_bytes=64) for lo, hi in gs_spans]
-        banks = [psum.tile([P, PASS], F32, name="bank%d" % b) for b in range(8)]
+        def kept(name, shape, dtype):
+            return keep.tile(shape, dtype, name=name, align_bytes=64)
+
+        ident = kept("ident", [P, P], F32)
+        x_sb = [kept("x%d" % n, [P, K], BF16) for n in range(TILES)]
+        force_w = [kept("force_w%d" % h, [P, PASSES, 2 * F], U8) for h in range(H)]
+        grasp_w = [kept("grasp_w%d" % h, [P, PASSES, 2 * N], U8) for h in range(H)]
+        force_planes = [kept("force_s%d" % lo, [P, PASSES * (hi - lo), F], U8) for lo, hi in FORCE_SCALE_SPANS]
+        grasp_planes = [kept("grasp_s%d" % lo, [P, PASSES * (hi - lo), N], U8) for lo, hi in GRASP_SCALE_SPANS]
+        bias_pairs = kept("bias_pairs", [P, H // 2, 8], F32)
+        bias_rows = [kept("bias_rows%d" % d, [P, 2 * F], BF16) for d in range(H // 2)]
+        wrench_sb = [kept("wrench%d" % h, [P, TILES_PER_OBJECT, N], BF16) for h in range(H)]
+        residual_sb = [kept("residual%d" % n, [P, N], F32) for n in range(TILES)]
+        cost_cols = kept("cost_cols", [P, QUADRANT], F32)
+        cost_rows = kept("cost_rows", [P, QUADRANT], F32)
+
+        banks = [psum.tile([P, PASS], F32, name="bank%d" % b) for b in range(BANKS)]
         taken = []
 
         def next_bank():
-            taken.append(banks[len(taken) % len(banks)])
+            taken.append(banks[len(taken) % BANKS])
             return taken[-1]
 
-        bias_sb = [keep.tile([P, F], BF16, name="bias%d" % h, align_bytes=64) for h in range(H)]
-        bw_first = keep.tile([P, G, 2], F32, name="bw_first", align_bytes=64)
-        bw_rest = keep.tile([P, (H - 1) * G, 2], F32, name="bw_rest", align_bytes=64)
-        wr_sb = [keep.tile([P, TILES_PER_OBJECT, N], BF16, name="wr%d" % h, align_bytes=64) for h in range(H)]
-        res_sb = [keep.tile([P, N], F32, name="res%d" % n, align_bytes=64) for n in range(TILES)]
-        cost_cols = keep.tile([P, 32], F32, name="cost_cols", align_bytes=64)
-        cost_rows = keep.tile([P, 32], F32, name="cost_rows", align_bytes=64)
+        def tiles_of(r):
+            return ROUNDS[r] if 0 <= r < len(ROUNDS) else []
 
-        def load_bias(queue, dst, rows):
-            queue.dma_start(out=dst[:], in_=rows.bitcast(F32).rearrange("h (c p u) -> p (h c) u", c=G, u=2))
+        def objects_starting_in(r):
+            return [n // TILES_PER_OBJECT for n in tiles_of(r) if n % TILES_PER_OBJECT == 0]
 
-        load_bias(nc.scalar, bw_first, bias[0:1, :])
+        nc.sync.dma_start(out=bias_pairs[:], in_=bias.bitcast(F32).rearrange("(d a) (b j) -> (a b) d j", a=2, j=8))
         make_identity(nc, ident[:])
-        for plane in (fs_sb[0], gs_sb[0], fs_sb[1], gs_sb[1], fs_sb[2]):
+        for plane in (force_planes[0], grasp_planes[0], force_planes[1], force_planes[2], grasp_planes[1]):
             nc.vector.memset(plane[:].bitcast(I32), 0)
-        nc.scalar.activation(out=cost_cols[:], in_=ident[:, 0:32], func=ACT.Square, scale=0.0)
+        nc.scalar.activation(out=cost_cols[:], in_=ident[:, 0:QUADRANT], func=ACT.Square, scale=0.0)
 
         def load_x(n):
             h, j = divmod(n, TILES_PER_OBJECT)
             nc.sync.dma_start(out=x_sb[n][:], in_=x[h, j * P : (j + 1) * P, :])
 
-        def load_words(dst, words, h, cols):
-            src = words[G * h : G * (h + 1), :, cols].rearrange("g p c -> p g c")
-            nc.sync.dma_start(out=dst[:, :, cols].bitcast(I32), in_=src.bitcast(I32))
+        def load_words(dst, words, h, byte_cols):
+            src = words[PASSES * h : PASSES * (h + 1), :, byte_cols].rearrange("g p c -> p g c")
+            nc.sync.dma_start(out=dst[:, :, byte_cols].bitcast(I32), in_=src.bitcast(I32))
 
-        def load_scales(planes, spans, scales, i):
-            lo, hi = spans[i]
-            for r in range(4):
-                src = scales[G * lo : G * hi, r:16:4, :].rearrange("g q n -> q g n")
-                nc.sync.dma_start(out=planes[i][r:P:32, :, :].bitcast(I32), in_=src.bitcast(I32))
+        def load_scales(planes, spans, scales, h):
+            for plane, (lo, hi) in zip(planes, spans):
+                if lo == h:
+                    for r in range(SCALE_ROWS):
+                        src = scales[PASSES * lo : PASSES * hi, r : P // 8 : SCALE_ROWS, :].rearrange("g q n -> q g n")
+                        nc.sync.dma_start(out=plane[r:P:QUADRANT, :, :].bitcast(I32), in_=src.bitcast(I32))
+
+        def load_force_weights(h):
+            first, *rest = [slice(0, F), slice(F, 2 * F)] if h == 0 else [slice(0, 2 * F)]
+            load_words(force_w[h], force_words, h, first)
+            load_scales(force_planes, FORCE_SCALE_SPANS, force_scales, h)
+            for byte_cols in rest:
+                load_words(force_w[h], force_words, h, byte_cols)
+
+        def load_grasp_weights(h):
+            load_words(grasp_w[h], grasp_words, h, slice(0, 2 * N))
+            load_scales(grasp_planes, GRASP_SCALE_SPANS, grasp_scales, h)
 
         def load_wrench(h):
-            nc.sync.dma_start(out=wr_sb[h][:], in_=wrench[h].rearrange("(j p) n -> p j n", p=P))
+            nc.sync.dma_start(out=wrench_sb[h][:], in_=wrench[h].rearrange("(j p) n -> p j n", p=P))
 
-        load_x(0)
-        load_x(1)
-        load_words(fw_sb[0], force_words, 0, slice(0, F))
-        load_scales(fs_sb, fs_spans, force_scales, 0)
-        load_words(fw_sb[0], force_words, 0, slice(F, 2 * F))
-        load_x(2)
-        load_bias(nc.sync, bw_rest, bias[1:, :])
-        load_x(3)
-        load_x(4)
-        load_words(gw_sb[0], grasp_words, 0, slice(0, 2 * N))
-        load_scales(gs_sb, gs_spans, grasp_scales, 0)
-        load_scales(fs_sb, fs_spans, force_scales, 1)
-        load_wrench(0)
-        load_x(5)
-        load_x(6)
-        load_words(fw_sb[1], force_words, 1, slice(0, 2 * F))
-        load_x(7)
-        load_x(8)
-        load_scales(gs_sb, gs_spans, grasp_scales, 1)
-        load_scales(fs_sb, fs_spans, force_scales, 2)
-        for h in range(1, H):
-            load_words(gw_sb[h], grasp_words, h, slice(0, 2 * N))
-            load_wrench(h)
-            if h + 1 < H:
-                load_words(fw_sb[h + 1], force_words, h + 1, slice(0, 2 * F))
-            for n in range(4 * h + 5, min(4 * h + 9, TILES)):
+        for r in range(-1, len(ROUNDS) + 3):
+            for n in tiles_of(r + 1):
                 load_x(n)
+            for h in objects_starting_in(r - 3):
+                load_wrench(h)
+            for h in objects_starting_in(r):
+                load_force_weights(h)
+            for h in objects_starting_in(r - 2):
+                load_grasp_weights(h)
 
-        bt = {}
-        xt = {}
-        xg = {}
-        xq = {}
-        pre = {}
-        fb = {}
-        ft = {}
-        fg = {}
-        fq = {}
-        acc = {}
+        bias_bank, x_bank, x_grouped, x_mx = {}, {}, {}, {}
+        sum_bank, sum_sb, force_bank, force_grouped, force_mx, applied_bank = {}, {}, {}, {}, {}, {}
 
         def plane_of(planes, spans, h, g):
             i = max(i for i, (lo, hi) in enumerate(spans) if lo <= h)
-            return planes[i][:, G * (h - spans[i][0]) + g, :]
+            return planes[i][:, PASSES * (h - spans[i][0]) + g, :]
 
-        def take_bank(passes):
-            bank = next_bank()
-            return bank[:, 0 : 2 * passes * P].rearrange("p (u g r) -> p u g r", u=2, g=passes)
-
-        whole = [(0, G)]
-        by_pass = [(0, 1), (1, 2)]
+        def pair_bank(passes):
+            return next_bank()[:, 0 : 2 * passes * P].rearrange("p (u g r) -> p u g r", u=2, g=passes)
 
         def x_groups(n):
-            return by_pass if n == 0 else whole
+            return PASS_BY_PASS if n == 0 else BOTH_PASSES
 
         def force_groups(n):
-            return by_pass if n == TILES - 1 else whole
+            return PASS_BY_PASS if n == TILES - 1 else BOTH_PASSES
 
-        def transpose_bias(h):
-            bt[h] = next_bank()
-            words = bw_first[:] if h == 0 else bw_rest[:, G * (h - 1) : G * h, :]
-            for c in range(G):
-                for u in range(2):
-                    column = words[:, c, u : u + 1].to_broadcast([P, P])
-                    nc.tensor.transpose(bt[h][:, (2 * c + u) * P : (2 * c + u + 1) * P], column, ident[:])
+        def spread_bias(d, u):
+            bias_bank[d, u] = next_bank()
+            for i in range(4):
+                column = bias_pairs[:, d, 2 * i + u : 2 * i + u + 1].to_broadcast([P, P])
+                nc.tensor.transpose(bias_bank[d, u][:, i * P : (i + 1) * P], column, ident[:])
 
-        def copy_bias(h):
-            nc.scalar.copy(out=bias_sb[h][:].bitcast(F32), in_=bt[h][:])
+        def copy_bias(d, u):
+            rows = bias_rows[d][:].bitcast(F32).rearrange("t (s u b i) -> t u s b i", s=4, u=2, i=4)
+            nc.scalar.copy(out=rows[:, u], in_=bias_bank[d, u][:].rearrange("t (i s b) -> t s b i", i=4, s=4))
 
         def transpose_x(n):
-            words = x_sb[n][:].bitcast(F32)
+            pairs = x_sb[n][:].bitcast(F32)
             for lo, hi in x_groups(n):
-                xt[n, lo] = take_bank(hi - lo)
+                x_bank[n, lo] = pair_bank(hi - lo)
                 for g in range(lo, hi):
                     for u in range(2):
                         nc.tensor.transpose(
-                            xt[n, lo][:, u, g - lo, :], words[:, 256 * g + u : 256 * (g + 1) : 2], ident[:]
+                            x_bank[n, lo][:, u, g - lo, :], pairs[:, PAIRS * g + u : PAIRS * (g + 1) : 2], ident[:]
                         )
 
         def copy_x(n):
-            xg[n] = work.tile([P, K], BF16, name="xg", align_bytes=64)
+            x_grouped[n] = work.tile([P, K], BF16, name="x_grouped", align_bytes=64)
             for lo, hi in x_groups(n):
                 nc.scalar.copy(
-                    out=xg[n][:, PASS * lo : PASS * hi].bitcast(F32).rearrange("p (w u) -> p w u", u=2),
-                    in_=xt[n, lo].rearrange("p u g r -> p (g r) u"),
+                    out=x_grouped[n][:, PASS * lo : PASS * hi].bitcast(F32).rearrange("p (w u) -> p w u", u=2),
+                    in_=x_bank[n, lo].rearrange("p u g r -> p (g r) u"),
                 )
 
-        def quantize(src, tag, groups):
-            codes = work.tile([P, G * P], U32, name=tag + "_codes", align_bytes=64)
-            scales = work.tile([P, G * P], U8, name=tag + "_scales", align_bytes=64)
+        def quantize(grouped, tag, groups):
+            codes = work.tile([P, PASSES * P], U32, name=tag + "_codes", align_bytes=64)
+            plane = work.tile([P, PASSES * P], U8, name=tag + "_plane", align_bytes=64)
             for lo, hi in groups:
                 nc.vector.quantize_mx(
                     out=codes[:, lo * P : hi * P].bitcast(FP8X4),
-                    scales=scales[:, lo * P : hi * P],
-                    in_=src[:, lo * PASS : hi * PASS],
+                    scales=plane[:, lo * P : hi * P],
+                    in_=grouped[:, lo * PASS : hi * PASS],
                 )
-            return codes, scales
+            return codes, plane
 
         def quantize_x(n):
-            xq[n] = quantize(xg[n], "xq", x_groups(n))
+            x_mx[n] = quantize(x_grouped[n], "x", x_groups(n))
 
         def matmul_force(n):
             h = n // TILES_PER_OBJECT
-            codes, scales = xq[n]
-            for c in range(G):
-                pre[n, c] = next_bank()
-                for g in range(G):
+            codes, plane = x_mx[n]
+            for c in range(PASSES):
+                sum_bank[n, c] = next_bank()
+                for g in range(PASSES):
                     nc.tensor.matmul_mx(
-                        out=pre[n, c][:],
+                        out=sum_bank[n, c][:],
                         lhsT=codes[:, g * P : (g + 1) * P].bitcast(FP8X4),
-                        lhsT_scale=scales[:, g * P : (g + 1) * P],
-                        rhs=fw_sb[h][:, g, 2 * PASS * c : 2 * PASS * (c + 1)].bitcast(FP4X4),
-                        rhs_scale=plane_of(fs_sb, fs_spans, h, g)[:, PASS * c : PASS * (c + 1)],
+                        lhsT_scale=plane[:, g * P : (g + 1) * P],
+                        rhs=force_w[h][:, g, 2 * PASS * c : 2 * PASS * (c + 1)].bitcast(FP4X4),
+                        rhs_scale=plane_of(force_planes, FORCE_SCALE_SPANS, h, g)[:, PASS * c : PASS * (c + 1)],
                         start=(g == 0),
-                        stop=(g == G - 1),
+                        stop=(g == PASSES - 1),
                     )
 
         def add_bias(n):
-            h = n // TILES_PER_OBJECT
-            for c in range(G):
-                fb[n, c] = work.tile([P, PASS], BF16, name="fb", align_bytes=64, bufs=8)
+            d, a = divmod(n // TILES_PER_OBJECT, 2)
+            for c in range(PASSES):
+                stretch = PASSES * a + c
+                sum_sb[n, c] = work.tile([P, PASS], BF16, name="sum_sb", align_bytes=64, bufs=SUM_BUFS)
                 nc.vector.tensor_tensor(
-                    out=fb[n, c][:].rearrange("t (u p e) -> t u p e", u=2, e=2),
-                    in0=pre[n, c][:].rearrange("t (p u e) -> t u p e", u=2, e=2),
-                    in1=bias_sb[h][:, PASS * c : PASS * (c + 1)].rearrange("t (u p e) -> t u p e", u=2, e=2),
+                    out=sum_sb[n, c][:].rearrange("t (u p e) -> t u p e", u=2, e=2),
+                    in0=sum_bank[n, c][:].rearrange("t (p u e) -> t u p e", u=2, e=2),
+                    in1=bias_rows[d][:, PASS * stretch : PASS * (stretch + 1)].rearrange(
+                        "t (u p e) -> t u p e", u=2, e=2
+                    ),
                     op=ALU.add,
                 )
 
         def transpose_force(n):
             for lo, hi in force_groups(n):
-                ft[n, lo] = take_bank(hi - lo)
+                force_bank[n, lo] = pair_bank(hi - lo)
                 for c in range(lo, hi):
-                    words = fb[n, c][:].bitcast(F32)
+                    pairs = sum_sb[n, c][:].bitcast(F32)
                     for u in range(2):
-                        nc.tensor.transpose(ft[n, lo][:, u, c - lo, :], words[:, P * u : P * (u + 1)], ident[:])
+                        nc.tensor.transpose(force_bank[n, lo][:, u, c - lo, :], pairs[:, P * u : P * (u + 1)], ident[:])
 
         def relu_force(n):
-            fg[n] = work.tile([P, F], BF16, name="fg", align_bytes=64)
+            force_grouped[n] = work.tile([P, F], BF16, name="force_grouped", align_bytes=64)
             for lo, hi in force_groups(n):
-                pairs = ft[n, lo].rearrange("p u c r -> p (u c r)").bitcast(BF16)
+                values = force_bank[n, lo].rearrange("p u c r -> p (u c r)").bitcast(BF16)
                 nc.scalar.activation(
-                    out=fg[n][:, PASS * lo : PASS * hi].rearrange("p (w u e) -> p w u e", u=2, e=2),
-                    in_=pairs.rearrange("p (u w e) -> p w u e", u=2, e=2),
+                    out=force_grouped[n][:, PASS * lo : PASS * hi].rearrange("p (w u e) -> p w u e", u=2, e=2),
+                    in_=values.rearrange("p (u w e) -> p w u e", u=2, e=2),
                     func=ACT.Relu,
                 )
 
         def quantize_force(n):
-            fq[n] = quantize(fg[n], "fq", force_groups(n))
+            force_mx[n] = quantize(force_grouped[n], "force", force_groups(n))
 
         def matmul_wrench(n):
             h = n // TILES_PER_OBJECT
-            codes, scales = fq[n]
-            acc[n] = next_bank()
-            for g in range(G):
+            codes, plane = force_mx[n]
+            applied_bank[n] = next_bank()
+            for g in range(PASSES):
                 nc.tensor.matmul_mx(
-                    out=acc[n][:],
+                    out=applied_bank[n][:],
                     lhsT=codes[:, g * P : (g + 1) * P].bitcast(FP8X4),
-                    lhsT_scale=scales[:, g * P : (g + 1) * P],
-                    rhs=gw_sb[h][:, g, :].bitcast(FP4X4),
-                    rhs_scale=plane_of(gs_sb, gs_spans, h, g),
+                    lhsT_scale=plane[:, g * P : (g + 1) * P],
+                    rhs=grasp_w[h][:, g, :].bitcast(FP4X4),
+                    rhs_scale=plane_of(grasp_planes, GRASP_SCALE_SPANS, h, g),
                     start=(g == 0),
-                    stop=(g == G - 1),
+                    stop=(g == PASSES - 1),
                 )
 
-        def residual(n):
+        def subtract_wrench(n):
             h, j = divmod(n, TILES_PER_OBJECT)
-            nc.vector.tensor_tensor(out=res_sb[n][:], in0=acc[n][:], in1=wr_sb[h][:, j, :], op=ALU.subtract)
-            nc.sync.dma_start(out=out_0[h, j * P : (j + 1) * P, :], in_=res_sb[n][:])
+            nc.vector.tensor_tensor(
+                out=residual_sb[n][:], in0=applied_bank[n][:], in1=wrench_sb[h][:, j, :], op=ALU.subtract
+            )
+            nc.sync.dma_start(out=out_0[h, j * P : (j + 1) * P, :], in_=residual_sb[n][:])
 
-        def square_sum(n):
+        def mean_square(n):
             squares = work.tile([P, N], BF16, name="squares", align_bytes=64)
             nc.scalar.activation(
                 out=squares[:],
-                in_=res_sb[n][:],
+                in_=residual_sb[n][:],
                 func=ACT.Square,
                 scale=math.sqrt(1.0 / N),
                 accum_out=cost_cols[:, n : n + 1],
             )
 
-        bias_at = {-1: 0, 1: 1, 2: 2, 3: 3}
+        bias_steps = {2 * d + u - 2: [(d, u)] for d in range(H // 2) for u in range(2)}
 
-        rounds = [[0], [1], [2]] + [[n, n + 1] for n in range(3, TILES - 3, 2)] + [[TILES - 3], [TILES - 2], [TILES - 1]]
+        def each(step, r):
+            for n in tiles_of(r):
+                step(n)
 
-        def at(step, r):
-            if 0 <= r < len(rounds):
-                for n in rounds[r]:
-                    step(n)
-
-        for it in range(-1, len(rounds) + 3):
-            at(transpose_x, it + 1)
-            if it in bias_at:
-                transpose_bias(bias_at[it])
-            at(transpose_force, it - 1)
-            at(copy_x, it + 1)
-            if it in bias_at:
-                copy_bias(bias_at[it])
-            at(relu_force, it - 1)
-            at(square_sum, it - 3)
-            at(quantize_x, it + 1)
-            for n in rounds[it] if 0 <= it < len(rounds) else []:
+        for r in range(-2, len(ROUNDS) + 3):
+            each(transpose_x, r + 1)
+            for d, u in bias_steps.get(r, []):
+                spread_bias(d, u)
+            each(transpose_force, r - 1)
+            each(copy_x, r + 1)
+            for d, u in bias_steps.get(r, []):
+                copy_bias(d, u)
+            each(relu_force, r - 1)
+            each(mean_square, r - 3)
+            each(quantize_x, r + 1)
+            for n in tiles_of(r):
                 matmul_force(n)
                 add_bias(n)
-            at(matmul_wrench, it - 2)
-            at(quantize_force, it - 1)
-            at(residual, it - 2)
+            each(matmul_wrench, r - 2)
+            each(quantize_force, r - 1)
+            each(subtract_wrench, r - 2)
 
         nc.vector.transpose(cost_rows[:], cost_cols[:])
         cost_out = out_1.rearrange("h (j t) -> (h j) t", t=P)
-        for b in range(4):
+        for b in range(P // QUADRANT):
             queue = nc.sync if b % 2 == 0 else nc.scalar
-            queue.dma_start(out=cost_out[:, 32 * b : 32 * (b + 1)], in_=cost_rows[32 * b : 32 * b + TILES, :])
+            queue.dma_start(
+                out=cost_out[:, QUADRANT * b : QUADRANT * (b + 1)],
+                in_=cost_rows[QUADRANT * b : QUADRANT * b + TILES, :],
+            )

import math
from contextlib import ExitStack

import concourse.mybir as mybir
from concourse.masks import make_identity

H, M, K, F, N = 4, 512, 1024, 1024, 512
FLOPS = 2 * H * M * K * F + 2 * H * M * F * N

F32 = mybir.dt.float32
BF16 = mybir.dt.bfloat16
I32 = mybir.dt.int32
U32 = mybir.dt.uint32
U8 = mybir.dt.uint8
FP8X4 = mybir.dt.float8_e4m3fn_x4
FP4X4 = mybir.dt.float4_e2m1fn_x4
ACT = mybir.ActivationFunctionType
ALU = mybir.AluOpType

P = 128
PASS = 512
PASSES = 2
PAIRS = PASS // 2
QUADRANT = 32
SCALE_ROWS = 4
BANKS = 8
TILES_PER_OBJECT = M // P
TILES = H * TILES_PER_OBJECT

SINGLE_ROUNDS_FIRST = 3
ROUNDS = (
    [[n] for n in range(SINGLE_ROUNDS_FIRST)]
    + [[n, n + 1] for n in range(SINGLE_ROUNDS_FIRST, TILES - 1, 2)]
    + [[TILES - 1]]
)

FORCE_SCALE_SPANS = [(0, 1), (1, 2), (2, H)]
GRASP_SCALE_SPANS = [(0, 1), (1, H)]

WORK_BUFS = 6
SUM_BUFS = 8

BOTH_PASSES = [(0, PASSES)]
PASS_BY_PASS = [(g, g + 1) for g in range(PASSES)]


def tile_grasp_wrench_residual_s14_kernel(
    tc, x, force_words, force_scales, bias, grasp_words, grasp_scales, wrench, out_0, out_1
):
    nc = tc.nc
    with ExitStack() as ctx:
        keep = ctx.enter_context(tc.tile_pool(name="keep", bufs=1))
        work = ctx.enter_context(tc.tile_pool(name="work", bufs=WORK_BUFS))
        psum = ctx.enter_context(tc.psum_pool(name="psum", bufs=1))
        ctx.enter_context(tc.manual_schedule())

        def kept(name, shape, dtype):
            return keep.tile(shape, dtype, name=name, align_bytes=64)

        ident = kept("ident", [P, P], F32)
        x_sb = [kept("x%d" % n, [P, K], BF16) for n in range(TILES)]
        force_w = [kept("force_w%d" % h, [P, PASSES, 2 * F], U8) for h in range(H)]
        grasp_w = [kept("grasp_w%d" % h, [P, PASSES, 2 * N], U8) for h in range(H)]
        force_planes = [kept("force_s%d" % lo, [P, PASSES * (hi - lo), F], U8) for lo, hi in FORCE_SCALE_SPANS]
        grasp_planes = [kept("grasp_s%d" % lo, [P, PASSES * (hi - lo), N], U8) for lo, hi in GRASP_SCALE_SPANS]
        bias_pairs = kept("bias_pairs", [P, H // 2, 8], F32)
        bias_rows = [kept("bias_rows%d" % d, [P, 2 * F], BF16) for d in range(H // 2)]
        wrench_sb = [kept("wrench%d" % h, [P, TILES_PER_OBJECT, N], BF16) for h in range(H)]
        residual_sb = [kept("residual%d" % n, [P, N], F32) for n in range(TILES)]
        cost_cols = kept("cost_cols", [P, QUADRANT], F32)
        cost_rows = kept("cost_rows", [P, QUADRANT], F32)

        banks = [psum.tile([P, PASS], F32, name="bank%d" % b) for b in range(BANKS)]
        taken = []

        def next_bank():
            taken.append(banks[len(taken) % BANKS])
            return taken[-1]

        def tiles_of(r):
            return ROUNDS[r] if 0 <= r < len(ROUNDS) else []

        def objects_starting_in(r):
            return [n // TILES_PER_OBJECT for n in tiles_of(r) if n % TILES_PER_OBJECT == 0]

        nc.sync.dma_start(out=bias_pairs[:], in_=bias.bitcast(F32).rearrange("(d a) (b j) -> (a b) d j", a=2, j=8))
        make_identity(nc, ident[:])
        for plane in (force_planes[0], grasp_planes[0], force_planes[1], force_planes[2], grasp_planes[1]):
            nc.vector.memset(plane[:].bitcast(I32), 0)
        nc.scalar.activation(out=cost_cols[:], in_=ident[:, 0:QUADRANT], func=ACT.Square, scale=0.0)

        def load_x(n):
            h, j = divmod(n, TILES_PER_OBJECT)
            nc.sync.dma_start(out=x_sb[n][:], in_=x[h, j * P : (j + 1) * P, :])

        def load_words(dst, words, h, byte_cols):
            src = words[PASSES * h : PASSES * (h + 1), :, byte_cols].rearrange("g p c -> p g c")
            nc.sync.dma_start(out=dst[:, :, byte_cols].bitcast(I32), in_=src.bitcast(I32))

        def load_scales(planes, spans, scales, h):
            for plane, (lo, hi) in zip(planes, spans):
                if lo == h:
                    for r in range(SCALE_ROWS):
                        src = scales[PASSES * lo : PASSES * hi, r : P // 8 : SCALE_ROWS, :].rearrange("g q n -> q g n")
                        nc.sync.dma_start(out=plane[r:P:QUADRANT, :, :].bitcast(I32), in_=src.bitcast(I32))

        def load_force_weights(h):
            first, *rest = [slice(0, F), slice(F, 2 * F)] if h == 0 else [slice(0, 2 * F)]
            load_words(force_w[h], force_words, h, first)
            load_scales(force_planes, FORCE_SCALE_SPANS, force_scales, h)
            for byte_cols in rest:
                load_words(force_w[h], force_words, h, byte_cols)

        def load_grasp_weights(h):
            load_words(grasp_w[h], grasp_words, h, slice(0, 2 * N))
            load_scales(grasp_planes, GRASP_SCALE_SPANS, grasp_scales, h)

        def load_wrench(h):
            nc.sync.dma_start(out=wrench_sb[h][:], in_=wrench[h].rearrange("(j p) n -> p j n", p=P))

        for r in range(-1, len(ROUNDS) + 3):
            for n in tiles_of(r + 1):
                load_x(n)
            for h in objects_starting_in(r - 3):
                load_wrench(h)
            for h in objects_starting_in(r):
                load_force_weights(h)
            for h in objects_starting_in(r - 2):
                load_grasp_weights(h)

        bias_bank, x_bank, x_grouped, x_mx = {}, {}, {}, {}
        sum_bank, sum_sb, force_bank, force_grouped, force_mx, applied_bank = {}, {}, {}, {}, {}, {}

        def plane_of(planes, spans, h, g):
            i = max(i for i, (lo, hi) in enumerate(spans) if lo <= h)
            return planes[i][:, PASSES * (h - spans[i][0]) + g, :]

        def pair_bank(passes):
            return next_bank()[:, 0 : 2 * passes * P].rearrange("p (u g r) -> p u g r", u=2, g=passes)

        def x_groups(n):
            return PASS_BY_PASS if n == 0 else BOTH_PASSES

        def force_groups(n):
            return PASS_BY_PASS if n == TILES - 1 else BOTH_PASSES

        def spread_bias(d, u):
            bias_bank[d, u] = next_bank()
            for i in range(4):
                column = bias_pairs[:, d, 2 * i + u : 2 * i + u + 1].to_broadcast([P, P])
                nc.tensor.transpose(bias_bank[d, u][:, i * P : (i + 1) * P], column, ident[:])

        def copy_bias(d, u):
            rows = bias_rows[d][:].bitcast(F32).rearrange("t (s u b i) -> t u s b i", s=4, u=2, i=4)
            nc.scalar.copy(out=rows[:, u], in_=bias_bank[d, u][:].rearrange("t (i s b) -> t s b i", i=4, s=4))

        def transpose_x(n):
            pairs = x_sb[n][:].bitcast(F32)
            for lo, hi in x_groups(n):
                x_bank[n, lo] = pair_bank(hi - lo)
                for g in range(lo, hi):
                    for u in range(2):
                        nc.tensor.transpose(
                            x_bank[n, lo][:, u, g - lo, :], pairs[:, PAIRS * g + u : PAIRS * (g + 1) : 2], ident[:]
                        )

        def copy_x(n):
            x_grouped[n] = work.tile([P, K], BF16, name="x_grouped", align_bytes=64)
            for lo, hi in x_groups(n):
                nc.scalar.copy(
                    out=x_grouped[n][:, PASS * lo : PASS * hi].bitcast(F32).rearrange("p (w u) -> p w u", u=2),
                    in_=x_bank[n, lo].rearrange("p u g r -> p (g r) u"),
                )

        def quantize(grouped, tag, groups):
            codes = work.tile([P, PASSES * P], U32, name=tag + "_codes", align_bytes=64)
            plane = work.tile([P, PASSES * P], U8, name=tag + "_plane", align_bytes=64)
            for lo, hi in groups:
                nc.vector.quantize_mx(
                    out=codes[:, lo * P : hi * P].bitcast(FP8X4),
                    scales=plane[:, lo * P : hi * P],
                    in_=grouped[:, lo * PASS : hi * PASS],
                )
            return codes, plane

        def quantize_x(n):
            x_mx[n] = quantize(x_grouped[n], "x", x_groups(n))

        def matmul_force(n):
            h = n // TILES_PER_OBJECT
            codes, plane = x_mx[n]
            for c in range(PASSES):
                sum_bank[n, c] = next_bank()
                for g in range(PASSES):
                    nc.tensor.matmul_mx(
                        out=sum_bank[n, c][:],
                        lhsT=codes[:, g * P : (g + 1) * P].bitcast(FP8X4),
                        lhsT_scale=plane[:, g * P : (g + 1) * P],
                        rhs=force_w[h][:, g, 2 * PASS * c : 2 * PASS * (c + 1)].bitcast(FP4X4),
                        rhs_scale=plane_of(force_planes, FORCE_SCALE_SPANS, h, g)[:, PASS * c : PASS * (c + 1)],
                        start=(g == 0),
                        stop=(g == PASSES - 1),
                    )

        def add_bias(n):
            d, a = divmod(n // TILES_PER_OBJECT, 2)
            for c in range(PASSES):
                stretch = PASSES * a + c
                sum_sb[n, c] = work.tile([P, PASS], BF16, name="sum_sb", align_bytes=64, bufs=SUM_BUFS)
                nc.vector.tensor_tensor(
                    out=sum_sb[n, c][:].rearrange("t (u p e) -> t u p e", u=2, e=2),
                    in0=sum_bank[n, c][:].rearrange("t (p u e) -> t u p e", u=2, e=2),
                    in1=bias_rows[d][:, PASS * stretch : PASS * (stretch + 1)].rearrange(
                        "t (u p e) -> t u p e", u=2, e=2
                    ),
                    op=ALU.add,
                )

        def transpose_force(n):
            for lo, hi in force_groups(n):
                force_bank[n, lo] = pair_bank(hi - lo)
                for c in range(lo, hi):
                    pairs = sum_sb[n, c][:].bitcast(F32)
                    for u in range(2):
                        nc.tensor.transpose(force_bank[n, lo][:, u, c - lo, :], pairs[:, P * u : P * (u + 1)], ident[:])

        def relu_force(n):
            force_grouped[n] = work.tile([P, F], BF16, name="force_grouped", align_bytes=64)
            for lo, hi in force_groups(n):
                values = force_bank[n, lo].rearrange("p u c r -> p (u c r)").bitcast(BF16)
                nc.scalar.activation(
                    out=force_grouped[n][:, PASS * lo : PASS * hi].rearrange("p (w u e) -> p w u e", u=2, e=2),
                    in_=values.rearrange("p (u w e) -> p w u e", u=2, e=2),
                    func=ACT.Relu,
                )

        def quantize_force(n):
            force_mx[n] = quantize(force_grouped[n], "force", force_groups(n))

        def matmul_wrench(n):
            h = n // TILES_PER_OBJECT
            codes, plane = force_mx[n]
            applied_bank[n] = next_bank()
            for g in range(PASSES):
                nc.tensor.matmul_mx(
                    out=applied_bank[n][:],
                    lhsT=codes[:, g * P : (g + 1) * P].bitcast(FP8X4),
                    lhsT_scale=plane[:, g * P : (g + 1) * P],
                    rhs=grasp_w[h][:, g, :].bitcast(FP4X4),
                    rhs_scale=plane_of(grasp_planes, GRASP_SCALE_SPANS, h, g),
                    start=(g == 0),
                    stop=(g == PASSES - 1),
                )

        def subtract_wrench(n):
            h, j = divmod(n, TILES_PER_OBJECT)
            nc.vector.tensor_tensor(
                out=residual_sb[n][:], in0=applied_bank[n][:], in1=wrench_sb[h][:, j, :], op=ALU.subtract
            )
            nc.sync.dma_start(out=out_0[h, j * P : (j + 1) * P, :], in_=residual_sb[n][:])

        def mean_square(n):
            squares = work.tile([P, N], BF16, name="squares", align_bytes=64)
            nc.scalar.activation(
                out=squares[:],
                in_=residual_sb[n][:],
                func=ACT.Square,
                scale=math.sqrt(1.0 / N),
                accum_out=cost_cols[:, n : n + 1],
            )

        bias_steps = {2 * d + u - 2: [(d, u)] for d in range(H // 2) for u in range(2)}

        def each(step, r):
            for n in tiles_of(r):
                step(n)

        for r in range(-2, len(ROUNDS) + 3):
            each(transpose_x, r + 1)
            for d, u in bias_steps.get(r, []):
                spread_bias(d, u)
            each(transpose_force, r - 1)
            each(copy_x, r + 1)
            for d, u in bias_steps.get(r, []):
                copy_bias(d, u)
            each(relu_force, r - 1)
            each(mean_square, r - 3)
            each(quantize_x, r + 1)
            for n in tiles_of(r):
                matmul_force(n)
                add_bias(n)
            each(matmul_wrench, r - 2)
            each(quantize_force, r - 1)
            each(subtract_wrench, r - 2)

        nc.vector.transpose(cost_rows[:], cost_cols[:])
        cost_out = out_1.rearrange("h (j t) -> (h j) t", t=P)
        for b in range(P // QUADRANT):
            queue = nc.sync if b % 2 == 0 else nc.scalar
            queue.dma_start(
                out=cost_out[:, QUADRANT * b : QUADRANT * (b + 1)],
                in_=cost_rows[QUADRANT * b : QUADRANT * b + TILES, :],
            )
